import numpy as np
import ml_dtypes


def mxq(x, axis, fmt="e4m3"):
    dtype, down = {"e4m3": (ml_dtypes.float8_e4m3fn, 7), "e5m2": (ml_dtypes.float8_e5m2, 14)}[fmt]
    v = np.moveaxis(np.asarray(x, np.float32).astype(ml_dtypes.bfloat16).astype(np.float64), axis, -1)
    blocks = v.reshape(v.shape[:-1] + (-1, 32))
    amax = np.abs(blocks).max(-1, keepdims=True)
    byte = np.maximum(np.where(amax > 0, np.frexp(amax)[1] - 1 + 127, 0) - down, 1)
    scale = np.exp2(byte - 127.0)
    codes = (blocks / scale).astype(np.float32).astype(dtype).astype(np.float64)
    return np.moveaxis((codes * scale).reshape(v.shape), -1, axis)


WIDE = False


def mx_kscale(k):
    if not WIDE:
        return np.ones(k)
    levels = np.array([10, -10, 5, -5, 0])
    if k % 512:
        return np.exp2(np.random.permutation(np.resize(levels, k // 32))).repeat(32)
    a = np.empty((k // 512, 16))
    for p in range(k // 512):
        a[p, :8] = np.random.permutation(np.resize(levels, 8))
        for g in range(8):
            far = levels[np.abs(levels - a[p, g]) >= 10]
            a[p, g + 8] = far[np.random.randint(len(far))]
    return np.exp2(a.ravel()).repeat(32)


BF16 = ml_dtypes.bfloat16


def bf(x):
    return np.asarray(x, np.float32).astype(BF16)


def f64(x):
    return np.asarray(x).astype(np.float64)


E2M1 = np.array([0.0, 0.5, 1.0, 1.5, 2.0, 3.0, 4.0, 6.0, -0.0, -0.5, -1.0, -1.5, -2.0, -3.0, -4.0, -6.0])


def pack_weight(w, fmt):
    k, n = w.shape
    w = f64(bf(w)).reshape(k // 32, 32, n)
    amax = np.abs(w).max(1)
    if fmt == "e4m3":
        byte = np.frexp(amax)[1] - 1 + 127 - 7
    else:
        mant, ex = np.frexp(amax / 6.0)
        byte = np.where(mant > 0.5, ex, ex - 1) + 127
    byte = np.clip(np.where(amax > 0, byte, 1), 1, 254)
    scaled = (w * np.exp2(127.0 - byte)[:, None, :]).reshape(k, n).astype(np.float32)
    by_word = np.ascontiguousarray(scaled.reshape(k // 512, 128, 4, n).transpose(0, 1, 3, 2))
    if fmt == "e4m3":
        words = by_word.astype(ml_dtypes.float8_e4m3fn).view(np.uint8)
    else:
        c = by_word.astype(ml_dtypes.float4_e2m1fn).view(np.uint8) & 0xF
        words = c[..., 0::2] | (c[..., 1::2] << 4)
    return np.ascontiguousarray(words), np.ascontiguousarray(byte.astype(np.uint8).reshape(k // 512, 16, n))


def unpack_weight(words, scales, fmt):
    g, p, n, _ = words.shape
    if fmt == "e4m3":
        vals = np.ascontiguousarray(words).view(ml_dtypes.float8_e4m3fn).astype(np.float64)
    else:
        nib = np.empty((g, p, n, 4), np.uint8)
        nib[..., 0::2] = words & 0xF
        nib[..., 1::2] = words >> 4
        vals = E2M1[nib]
    vals = vals * np.repeat(np.exp2(scales.astype(np.float64) - 127.0), 8, axis=1)[..., None]
    return vals.transpose(0, 1, 3, 2).reshape(g * 512, n)
def pack4(w):
    words, scales = pack_weight(w, "e2m1")
    return words.reshape(words.shape[0], 128, -1), scales


def unpack4(words, scales):
    return unpack_weight(words.reshape(words.shape[0], 128, -1, 2), scales, "e2m1")


S, Z, F = 1024, 1536, 512


def setup_inputs():
    u, v = mx_kscale(Z), mx_kscale(S)
    stocks = bf(np.random.standard_normal((S, Z)) * v[:, None] * u)
    move = np.random.standard_normal((Z, Z)) / (3 * np.sqrt(Z)) / u[:, None] * u
    prey = np.random.standard_normal((S, S)) / (3 * np.sqrt(S)) / v[:, None] * v
    effort = np.random.standard_normal((Z, F)) / np.sqrt(Z) / u[:, None]
    move_words, move_scales = pack4(move)
    prey_words, prey_scales = pack4(prey)
    effort_words, effort_scales = pack4(effort)
    return {"stocks": stocks,
            "move_words": move_words, "move_scales": move_scales,
            "mobility": bf(1 + 0.1 * np.random.standard_normal(S)),
            "prey_words": prey_words, "prey_scales": prey_scales,
            "overlap": bf(1 + 0.1 * np.random.standard_normal(Z)),
            "effort_words": effort_words, "effort_scales": effort_scales,
            "catchability": bf((1 + 0.1 * np.random.standard_normal((S, F))) / v[:, None])}


def reference(stocks, move_words, move_scales, mobility, prey_words, prey_scales, overlap, effort_words, effort_scales, catchability):
    x = f64(stocks)
    moved = mxq(x, 1, "e4m3") @ unpack4(move_words, move_scales)
    h1 = x + f64(mobility)[:, None] * moved
    eaten = unpack4(prey_words, prey_scales).T @ mxq(h1, 0, "e4m3")
    h2 = h1 + f64(overlap) * eaten
    exposure = mxq(h2, 1, "e4m3") @ unpack4(effort_words, effort_scales)
    return f64(catchability) * exposure

@@ -1,0 +1,424 @@
+from contextlib import ExitStack
+
+import concourse.mybir as mybir
+from concourse.masks import make_identity
+
+FLOPS = 2 * 1024 * 1536 * 1536 + 2 * 1024 * 1024 * 1536 + 2 * 1024 * 1536 * 512
+
+F32 = mybir.dt.float32
+BF16 = mybir.dt.bfloat16
+I32 = mybir.dt.int32
+U32 = mybir.dt.uint32
+U8 = mybir.dt.uint8
+FP8X4 = mybir.dt.float8_e4m3fn_x4
+FP4X4 = mybir.dt.float4_e2m1fn_x4
+MULT = mybir.AluOpType.mult
+ADD = mybir.AluOpType.add
+COPY = mybir.ActivationFunctionType.Copy
+
+P = 128
+NC = 3
+NI = 8
+NF = 512
+
+
+def tile_fish_zone_bycatch_t2_kernel(
+    tc, stocks, move_words, move_scales, mobility, prey_words, prey_scales, overlap,
+    effort_words, effort_scales, catchability, out,
+):
+    nc = tc.nc
+    with ExitStack() as ctx:
+        keep = ctx.enter_context(tc.tile_pool(name="keep", bufs=1))
+        work = ctx.enter_context(tc.tile_pool(name="work", bufs=2))
+        psum = ctx.enter_context(tc.psum_pool(name="psum", bufs=8))
+
+        def bank():
+            t = psum.tile([P, 512], F32, name="bank")
+            return t
+
+        ctx.enter_context(tc.manual_schedule())
+
+        ident = keep.tile([P, P], F32, name="ident", align_bytes=64)
+        x_sb = [keep.tile([P, 1536], BF16, name="x%d" % i, align_bytes=64) for i in range(NI)]
+        x_codes = [keep.tile([P, 384], U32, name="xc%d" % i, align_bytes=64) for i in range(NI)]
+        x_sc = [keep.tile([P, 384], U8, name="xs%d" % i, align_bytes=64) for i in range(NI)]
+        a_w = [keep.tile([P, 3072], U8, name="aw%d" % c, align_bytes=64) for c in range(NC)]
+        a_s = keep.tile([P, 4608], U8, name="a_s", align_bytes=64)
+        b_w = keep.tile([P, 4096], U8, name="b_w", align_bytes=64)
+        b_s = keep.tile([P, 2048], U8, name="b_s", align_bytes=64)
+        e_w = keep.tile([P, 3072], U8, name="e_w", align_bytes=64)
+        e_s = keep.tile([P, 1536], U8, name="e_s", align_bytes=64)
+        mob_b = keep.tile([P, NI], BF16, name="mob_b")
+        ov_b = keep.tile([P, 12], BF16, name="ov_b")
+        mob = keep.tile([P, NI], F32, name="mob")
+        ov = keep.tile([P, 12], F32, name="ov")
+        catch = keep.tile([P, NI * NF], BF16, name="catch", align_bytes=64)
+        h1_codes = {}
+        h1_sc = {}
+        h2_codes = {}
+        h2_sc = {}
+        for c in range(NC):
+            for h in range(2):
+                h1_codes[c, h] = keep.tile([P, 512], U32, name="h1c%d%d" % (c, h), align_bytes=64)
+                h1_sc[c, h] = keep.tile([P, 512], U8, name="h1s%d%d" % (c, h), align_bytes=64)
+            h2_codes[c] = keep.tile([P, 1024], U32, name="h2c%d" % c, align_bytes=64)
+            h2_sc[c] = keep.tile([P, 1024], U8, name="h2s%d" % c, align_bytes=64)
+
+        x_view = stocks.rearrange("(h p t) z -> h t p z", p=P, t=4)
+        aw_view = move_words.bitcast(I32).rearrange("g p w -> p g w")
+        bw_view = prey_words.bitcast(I32).rearrange("g p w -> p g w")
+        ew_view = effort_words.bitcast(I32).rearrange("g p w -> p g w")
+
+        def load_x(i):
+            nc.sync.dma_start(out=x_sb[i][:], in_=x_view[i // 4, i % 4])
+
+        def load_a(c):
+            nc.sync.dma_start(
+                out=a_w[c][:].bitcast(I32).rearrange("p (g w) -> p g w", g=3),
+                in_=aw_view[:, :, 256 * c : 256 * (c + 1)],
+            )
+
+        def load_scales(queue, plane, scales, groups):
+            src = scales.bitcast(I32).rearrange("g r w -> r g w")
+            for q in range(4):
+                queue.dma_start(
+                    out=plane[32 * q : 32 * q + 4, :].bitcast(I32).rearrange("r (g w) -> r g w", g=groups),
+                    in_=src[4 * q : 4 * q + 4],
+                )
+
+        nc.vector.memset(a_s[:].bitcast(U32), 0)
+        nc.gpsimd.memset(b_s[:].bitcast(U32), 0)
+        nc.gpsimd.memset(e_s[:].bitcast(U32), 0)
+        make_identity(nc, ident[:])
+        for g in range(3):
+            nc.sync.dma_start(out=x_sb[0][:, 512 * g : 512 * (g + 1)], in_=x_view[0, 0][:, 512 * g : 512 * (g + 1)])
+        load_x(1)
+        load_scales(nc.scalar, a_s, move_scales, 3)
+        nc.scalar.dma_start(
+            out=mob_b[:].rearrange("p (h t) -> p h t", h=2),
+            in_=mobility.rearrange("(h p t) -> p h t", p=P, t=4),
+        )
+        load_a(0)
+        for i in range(2, NI):
+            load_x(i)
+        nc.sync.dma_start(
+            out=ov_b[:].rearrange("p (c t) -> p c t", c=3),
+            in_=overlap.rearrange("(c p t) -> p c t", p=P, t=4),
+        )
+        load_a(1)
+        nc.sync.dma_start(out=b_w[:].bitcast(I32).rearrange("p (g w) -> p g w", g=2), in_=bw_view)
+        load_scales(nc.sync, b_s, prey_scales, 2)
+        load_a(2)
+        load_scales(nc.sync, e_s, effort_scales, 3)
+        nc.sync.dma_start(out=e_w[:].bitcast(I32).rearrange("p (g w) -> p g w", g=3), in_=ew_view)
+        nc.sync.dma_start(
+            out=catch[:].rearrange("p (j f) -> p j f", j=NI),
+            in_=catchability.rearrange("(j p) f -> p j f", p=P),
+        )
+
+        nc.gpsimd.tensor_copy(out=mob[:], in_=mob_b[:])
+        nc.gpsimd.tensor_copy(out=ov[:], in_=ov_b[:])
+
+        xw = {}
+        xbank = {}
+        xg = {}
+
+        def permute_x(i, lo, hi):
+            if lo == 0:
+                t = work.tile([P, 2, 384], F32, name="xw", align_bytes=64, bufs=4)
+                xw[i] = t
+            nc.vector.tensor_copy(
+                out=xw[i][:, :, 128 * lo : 128 * hi],
+                in_=x_sb[i][:, 512 * lo : 512 * hi].bitcast(F32).rearrange("s (w u) -> s u w", u=2),
+            )
+
+        def transpose_x(i):
+            j = i % 2
+            if j == 0:
+                xbank["shared"] = bank()
+            xbank[i] = (bank(), xbank["shared"])
+            for g in range(3):
+                for u in range(2):
+                    if g < 2:
+                        dst = xbank[i][0][:, 256 * g + 128 * u : 256 * g + 128 * (u + 1)]
+                    else:
+                        dst = xbank[i][1][:, 256 * j + 128 * u : 256 * j + 128 * (u + 1)]
+                    nc.tensor.transpose(dst, xw[i][:, u, 128 * g : 128 * (g + 1)], ident[:])
+
+        def copy_x(i, part, engine):
+            if part == 0:
+                t = work.tile([P, 1536], BF16, name="xg", align_bytes=64, bufs=4)
+                xg[i] = t
+                dst = t[:, :1024].bitcast(F32).rearrange("z (g s u) -> z g s u", g=2, u=2)
+                src = xbank[i][0][:].rearrange("z (g u s) -> z g s u", g=2, u=2)
+            else:
+                dst = xg[i][:, 1024:].bitcast(F32).rearrange("z (s u) -> z s u", u=2)
+                src = xbank[i][1][:, 256 * (i % 2) : 256 * (i % 2) + 256].rearrange("z (u s) -> z s u", u=2)
+            if engine == "v":
+                nc.vector.tensor_copy(out=dst, in_=src)
+            else:
+                nc.scalar.copy(out=dst, in_=src)
+
+        def quant(codes, scales, src):
+            nc.vector.quantize_mx(out=codes.bitcast(FP8X4), scales=scales, in_=src)
+
+        def quant_x(i):
+            for lo, hi in ((0, 256), (256, 384)):
+                quant(x_codes[i][:, lo:hi], x_sc[i][:, lo:hi], xg[i][:, 4 * lo : 4 * hi])
+
+        s1 = {}
+        hf = {}
+        hg = {}
+
+        def move(c, i):
+            ps = bank()
+            for g in range(3):
+                cols = slice(128 * g, 128 * (g + 1))
+                nc.tensor.matmul_mx(
+                    out=ps[:],
+                    lhsT=x_codes[i][:, cols].bitcast(FP8X4),
+                    lhsT_scale=x_sc[i][:, cols],
+                    rhs=a_w[c][:, 1024 * g : 1024 * (g + 1)].bitcast(FP4X4),
+                    rhs_scale=a_s[:, 1536 * g + 512 * c : 1536 * g + 512 * (c + 1)],
+                    start=(g == 0),
+                    stop=(g == 2),
+                )
+            s1[c, i] = ps
+
+        def h1(c, i):
+            h, t = divmod(i, 4)
+            if t == 0:
+                full = work.tile([P, 2048], F32, name="hf", align_bytes=64, bufs=4)
+                hf[c, h] = full
+            nc.vector.scalar_tensor_tensor(
+                out=hf[c, h][:, 512 * t : 512 * (t + 1)].rearrange("s (t p) -> s t p", t=4),
+                in0=s1[c, i][:].rearrange("s (p t) -> s t p", t=4),
+                scalar=mob[:, i : i + 1],
+                in1=x_sb[i][:, 512 * c : 512 * (c + 1)].rearrange("s (p t) -> s t p", t=4),
+                op0=MULT,
+                op1=ADD,
+            )
+
+        def group_h1(c, h, q, engine="s"):
+            if q == 0:
+                t = work.tile([P, 2048], BF16, name="hg", align_bytes=64, bufs=2)
+                hg[c, h] = t
+            dst = hg[c, h][:, 512 * q : 512 * (q + 1)].rearrange("s (z t) -> s z t", t=4)
+            src = hf[c, h][:].rearrange("s (t z) -> s z t", t=4)[:, 128 * q : 128 * (q + 1), :]
+            if engine == "v":
+                nc.vector.tensor_copy(out=dst, in_=src)
+            else:
+                nc.scalar.copy(out=dst, in_=src)
+
+        def quant_h1(c, h, lo, hi):
+            cols = slice(128 * lo, 128 * hi)
+            quant(h1_codes[c, h][:, cols], h1_sc[c, h][:, cols], hg[c, h][:, 512 * lo : 512 * hi])
+
+        tb = {}
+        ht = {}
+
+        def transpose_h1(c, i):
+            h, t = divmod(i, 4)
+            ps = bank()
+            for tz in range(4):
+                nc.tensor.transpose(
+                    ps[:, 128 * tz : 128 * (tz + 1)],
+                    hf[c, h][:, 512 * t + 128 * tz : 512 * t + 128 * (tz + 1)],
+                    ident[:],
+                )
+            tb[c, i] = ps
+
+        def copy_h1(c, i, engine):
+            h, t = divmod(i, 4)
+            if (c, h) not in ht:
+                full = work.tile([P, 2048], F32, name="ht", align_bytes=64, bufs=4)
+                ht[c, h] = full
+            dst = ht[c, h][:].rearrange("z (p t q) -> z t p q", t=4, q=4)[:, t]
+            src = tb[c, i][:].rearrange("z (q p) -> z p q", q=4)
+            if engine == "v":
+                nc.vector.tensor_copy(out=dst, in_=src)
+            else:
+                nc.scalar.copy(out=dst, in_=src)
+
+        s2 = {}
+        eaten = {}
+        h2b = {}
+
+        def prey(c, half, q):
+            ps = bank()
+            for g in range(2):
+                nc.tensor.matmul_mx(
+                    out=ps[:],
+                    lhsT=h1_codes[c, g][:, 128 * q : 128 * (q + 1)].bitcast(FP8X4),
+                    lhsT_scale=h1_sc[c, g][:, 128 * q : 128 * (q + 1)],
+                    rhs=b_w[:, 2048 * g + 1024 * half : 2048 * g + 1024 * (half + 1)].bitcast(FP4X4),
+                    rhs_scale=b_s[:, 1024 * g + 512 * half : 1024 * g + 512 * (half + 1)],
+                    start=(g == 0),
+                    stop=(g == 1),
+                )
+            s2[c, half, q] = ps
+
+        def scale_eaten(c, half, q):
+            if q == 0:
+                t = work.tile([P, 2048], F32, name="eaten", align_bytes=64, bufs=2)
+                eaten[c, half] = t
+            nc.scalar.activation(
+                out=eaten[c, half][:, 512 * q : 512 * (q + 1)],
+                in_=s2[c, half, q][:],
+                func=COPY,
+                scale=ov[:, 4 * c + q : 4 * c + q + 1],
+            )
+
+        def prey_narrow(c, j):
+            ps = bank()
+            for q in range(4):
+                for g in range(2):
+                    nc.tensor.matmul_mx(
+                        out=ps[:, 128 * q : 128 * (q + 1)],
+                        lhsT=h1_codes[c, g][:, 128 * q : 128 * (q + 1)].bitcast(FP8X4),
+                        lhsT_scale=h1_sc[c, g][:, 128 * q : 128 * (q + 1)],
+                        rhs=b_w[:, 2048 * g + 256 * j : 2048 * g + 256 * (j + 1)].bitcast(FP4X4),
+                        rhs_scale=b_s[:, 1024 * g + 128 * j : 1024 * g + 128 * (j + 1)],
+                        start=(g == 0),
+                        stop=(g == 1),
+                    )
+            s2[c, j] = ps
+
+        def scale_narrow(c, j):
+            half, n = divmod(j, 4)
+            if n == 0:
+                t = work.tile([P, 2048], F32, name="eaten", align_bytes=64, bufs=2)
+                eaten[c, half] = t
+            for q in range(4):
+                nc.scalar.activation(
+                    out=eaten[c, half][:, 512 * q + 128 * n : 512 * q + 128 * (n + 1)],
+                    in_=s2[c, j][:, 128 * q : 128 * (q + 1)],
+                    func=COPY,
+                    scale=ov[:, 4 * c + q : 4 * c + q + 1],
+                )
+
+        def h2(c, half, n0, n):
+            t = work.tile([P, 1024], BF16, name="h2b", align_bytes=64, bufs=3)
+            nc.vector.tensor_tensor(
+                out=t[:, : 4 * n].rearrange("z (s q) -> z s q", q=4),
+                in0=eaten[c, half][:].rearrange("z (q s) -> z s q", q=4)[:, n0 : n0 + n, :],
+                in1=ht[c, half][:, 4 * n0 : 4 * (n0 + n)].rearrange("z (s q) -> z s q", q=4),
+                op=ADD,
+            )
+            h2b[c, half, n0] = t
+
+        def quant_h2(c, half, n0, n):
+            cols = slice(512 * half + n0, 512 * half + n0 + n)
+            quant(h2_codes[c][:, cols], h2_sc[c][:, cols], h2b[c, half, n0][:, : 4 * n])
+
+        s3 = {}
+
+        def expose(j, c):
+            if c == 0:
+                s3[j] = bank()
+            nc.tensor.matmul_mx(
+                out=s3[j][:],
+                lhsT=h2_codes[c][:, 128 * j : 128 * (j + 1)].bitcast(FP8X4),
+                lhsT_scale=h2_sc[c][:, 128 * j : 128 * (j + 1)],
+                rhs=e_w[:, 1024 * c : 1024 * (c + 1)].bitcast(FP4X4),
+                rhs_scale=e_s[:, 512 * c : 512 * (c + 1)],
+                start=(c == 0),
+                stop=(c == 2),
+            )
+
+        def finish(j):
+            t = work.tile([P, NF], F32, name="res", align_bytes=64, bufs=4)
+            nc.vector.tensor_tensor(out=t[:], in0=s3[j][:], in1=catch[:, NF * j : NF * (j + 1)], op=MULT)
+            nc.sync.dma_start(out=out[P * j : P * (j + 1), :], in_=t[:])
+
+        plan = {}
+
+        def at(step, stage, fn, *args):
+            plan.setdefault((step, stage), []).append((fn, args))
+
+        for c in range(NC):
+            for k in range(NI):
+                s = NI * c + k
+                at(s, "move", move, c, k)
+                at(s, "h1", h1, c, k)
+            for h in range(2):
+                s = NI * c + 4 * h + 3
+                for q in range(4):
+                    at(s + 1 + q // 2, "group", group_h1, c, h, q, "s")
+                at(s + 2, "quant", quant_h1, c, h, 0, 2)
+                at(s + 3, "quant", quant_h1, c, h, 2, 4)
+        TURN = (11, 15, 19, 24, 28, 32)
+        FIRST = 20
+        for u in range(6):
+            c, half = divmod(u, 2)
+            for t in range(4):
+                at(TURN[u], "turn", transpose_h1, c, 4 * half + t)
+                at(TURN[u], "copy", copy_h1, c, 4 * half + t, "v" if t % 2 and u > 2 else "s")
+            if u < 4:
+                for q in range(4):
+                    s = FIRST + 4 * u + q
+                    at(s, "prey", prey, c, half, q)
+                    at(s, "eaten", scale_eaten, c, half, q)
+                at(s + 1, "h2", h2, c, half, 0, 256)
+                at(s + 2, "h2", h2, c, half, 256, 256)
+                at(s + 2, "h2", quant_h2, c, half, 0, 256)
+                at(s + 3, "h2", quant_h2, c, half, 256, 256)
+
+        def emit(step):
+            for stage in ("turn", "move", "prey", "copy", "group", "eaten", "h2", "h1", "quant"):
+                for fn, args in plan.get((step, stage), []):
+                    fn(*args)
+
+        for g in range(3):
+            permute_x(0, g, g + 1)
+        permute_x(1, 0, 3)
+        transpose_x(0)
+        transpose_x(1)
+        copy_x(0, 0, "s")
+        copy_x(0, 1, "v")
+        copy_x(1, 0, "s")
+        quant_x(0)
+        copy_x(1, 1, "s")
+        permute_x(2, 0, 3)
+        permute_x(3, 0, 3)
+        quant_x(1)
+        emit(0)
+        for n, runs in ((2, (1,)), (4, (2,)), (6, (3, 4))):
+            for i in (n, n + 1):
+                transpose_x(i)
+            for i in (n, n + 1):
+                copy_x(i, 0, "s")
+                copy_x(i, 1, "s")
+            if n < 6:
+                permute_x(n + 2, 0, 3)
+                permute_x(n + 3, 0, 3)
+            for s in runs:
+                emit(s)
+            quant_x(n)
+            quant_x(n + 1)
+        for s in range(5, FIRST + 16):
+            emit(s)
+        PRE = 2
+        for j in range(PRE):
+            prey_narrow(2, j)
+            scale_narrow(2, j)
+        for j in range(8):
+            if j < 3:
+                emit(FIRST + 16 + j)
+            if j + PRE < 8:
+                prey_narrow(2, j + PRE)
+                scale_narrow(2, j + PRE)
+            expose(j, 0)
+            expose(j, 1)
+            if j >= 2:
+                expose(j - 2, 2)
+            h2(2, j // 4, 128 * (j % 4), 128)
+            if j > 0:
+                quant_h2(2, (j - 1) // 4, 128 * ((j - 1) % 4), 128)
+            if j >= 3:
+                finish(j - 3)
+        quant_h2(2, 1, 384, 128)
+        for j in (6, 7):
+            expose(j, 2)
+        for j in (5, 6, 7):
+            finish(j)

@@ -64,6 +64,8 @@ def tile_fish_zone_bycatch_t2_kernel(
             h2_codes[c] = keep.tile([P, 1024], U32, name="h2c%d" % c, align_bytes=64)
             h2_sc[c] = keep.tile([P, 1024], U8, name="h2s%d" % c, align_bytes=64)
 
+        out_view = out.rearrange("(h p t) f -> h t p f", p=P, t=4)
+
         x_view = stocks.rearrange("(h p t) z -> h t p z", p=P, t=4)
         aw_view = move_words.bitcast(I32).rearrange("g p w -> p g w")
         bw_view = prey_words.bitcast(I32).rearrange("g p w -> p g w")
@@ -112,8 +114,8 @@ def tile_fish_zone_bycatch_t2_kernel(
         load_scales(nc.sync, e_s, effort_scales, 3)
         nc.sync.dma_start(out=e_w[:].bitcast(I32).rearrange("p (g w) -> p g w", g=3), in_=ew_view)
         nc.sync.dma_start(
-            out=catch[:].rearrange("p (j f) -> p j f", j=NI),
-            in_=catchability.rearrange("(j p) f -> p j f", p=P),
+            out=catch[:].rearrange("p (h w) -> p h w", h=2),
+            in_=catchability.rearrange("(h p t) f -> p h (t f)", p=P, t=4),
         )
 
         nc.gpsimd.tensor_copy(out=mob[:], in_=mob_b[:])
@@ -188,7 +190,7 @@ def tile_fish_zone_bycatch_t2_kernel(
         def h1(c, i):
             h, t = divmod(i, 4)
             if t == 0:
-                full = work.tile([P, 2048], F32, name="hf", align_bytes=64, bufs=4)
+                full = work.tile([P, 2048], F32, name="hf", align_bytes=64, bufs=6)
                 hf[c, h] = full
             nc.vector.scalar_tensor_tensor(
                 out=hf[c, h][:, 512 * t : 512 * (t + 1)].rearrange("s (t p) -> s t p", t=4),
@@ -215,7 +217,6 @@ def tile_fish_zone_bycatch_t2_kernel(
             quant(h1_codes[c, h][:, cols], h1_sc[c, h][:, cols], hg[c, h][:, 512 * lo : 512 * hi])
 
         tb = {}
-        ht = {}
 
         def transpose_h1(c, i):
             h, t = divmod(i, 4)
@@ -227,18 +228,6 @@ def tile_fish_zone_bycatch_t2_kernel(
                     ident[:],
                 )
             tb[c, i] = ps
-
-        def copy_h1(c, i, engine):
-            h, t = divmod(i, 4)
-            if (c, h) not in ht:
-                full = work.tile([P, 2048], F32, name="ht", align_bytes=64, bufs=4)
-                ht[c, h] = full
-            dst = ht[c, h][:].rearrange("z (p t q) -> z t p q", t=4, q=4)[:, t]
-            src = tb[c, i][:].rearrange("z (q p) -> z p q", q=4)
-            if engine == "v":
-                nc.vector.tensor_copy(out=dst, in_=src)
-            else:
-                nc.scalar.copy(out=dst, in_=src)
 
         s2 = {}
         eaten = {}
@@ -260,56 +249,29 @@ def tile_fish_zone_bycatch_t2_kernel(
 
         def scale_eaten(c, half, q):
             if q == 0:
-                t = work.tile([P, 2048], F32, name="eaten", align_bytes=64, bufs=2)
+                t = work.tile([P, 2048], F32, name="eaten", align_bytes=64, bufs=3)
                 eaten[c, half] = t
             nc.scalar.activation(
-                out=eaten[c, half][:, 512 * q : 512 * (q + 1)],
-                in_=s2[c, half, q][:],
+                out=eaten[c, half][:, 512 * q : 512 * (q + 1)].rearrange("z (t p) -> z t p", t=4),
+                in_=s2[c, half, q][:].rearrange("z (p t) -> z t p", t=4),
                 func=COPY,
                 scale=ov[:, 4 * c + q : 4 * c + q + 1],
             )
 
-        def prey_narrow(c, j):
-            ps = bank()
-            for q in range(4):
-                for g in range(2):
-                    nc.tensor.matmul_mx(
-                        out=ps[:, 128 * q : 128 * (q + 1)],
-                        lhsT=h1_codes[c, g][:, 128 * q : 128 * (q + 1)].bitcast(FP8X4),
-                        lhsT_scale=h1_sc[c, g][:, 128 * q : 128 * (q + 1)],
-                        rhs=b_w[:, 2048 * g + 256 * j : 2048 * g + 256 * (j + 1)].bitcast(FP4X4),
-                        rhs_scale=b_s[:, 1024 * g + 128 * j : 1024 * g + 128 * (j + 1)],
-                        start=(g == 0),
-                        stop=(g == 1),
-                    )
-            s2[c, j] = ps
-
-        def scale_narrow(c, j):
-            half, n = divmod(j, 4)
-            if n == 0:
-                t = work.tile([P, 2048], F32, name="eaten", align_bytes=64, bufs=2)
-                eaten[c, half] = t
-            for q in range(4):
-                nc.scalar.activation(
-                    out=eaten[c, half][:, 512 * q + 128 * n : 512 * q + 128 * (n + 1)],
-                    in_=s2[c, j][:, 128 * q : 128 * (q + 1)],
-                    func=COPY,
-                    scale=ov[:, 4 * c + q : 4 * c + q + 1],
-                )
-
-        def h2(c, half, n0, n):
-            t = work.tile([P, 1024], BF16, name="h2b", align_bytes=64, bufs=3)
+        def h2(c, i):
+            half, t = divmod(i, 4)
+            tile = work.tile([P, 512], BF16, name="h2b", align_bytes=64, bufs=4)
             nc.vector.tensor_tensor(
-                out=t[:, : 4 * n].rearrange("z (s q) -> z s q", q=4),
-                in0=eaten[c, half][:].rearrange("z (q s) -> z s q", q=4)[:, n0 : n0 + n, :],
-                in1=ht[c, half][:, 4 * n0 : 4 * (n0 + n)].rearrange("z (s q) -> z s q", q=4),
+                out=tile[:].rearrange("z (p q) -> z p q", q=4),
+                in0=tb[c, i][:].rearrange("z (q p) -> z p q", q=4),
+                in1=eaten[c, half][:].rearrange("z (q t p) -> z t p q", q=4, t=4)[:, t],
                 op=ADD,
             )
-            h2b[c, half, n0] = t
+            h2b[c, i] = tile
 
-        def quant_h2(c, half, n0, n):
-            cols = slice(512 * half + n0, 512 * half + n0 + n)
-            quant(h2_codes[c][:, cols], h2_sc[c][:, cols], h2b[c, half, n0][:, : 4 * n])
+        def quant_h2(c, i):
+            cols = slice(128 * i, 128 * (i + 1))
+            quant(h2_codes[c][:, cols], h2_sc[c][:, cols], h2b[c, i][:])
 
         s3 = {}
 
@@ -327,9 +289,9 @@ def tile_fish_zone_bycatch_t2_kernel(
             )
 
         def finish(j):
-            t = work.tile([P, NF], F32, name="res", align_bytes=64, bufs=4)
+            t = work.tile([P, NF], F32, name="res", align_bytes=64, bufs=8)
             nc.vector.tensor_tensor(out=t[:], in0=s3[j][:], in1=catch[:, NF * j : NF * (j + 1)], op=MULT)
-            nc.sync.dma_start(out=out[P * j : P * (j + 1), :], in_=t[:])
+            nc.sync.dma_start(out=out_view[j // 4, j % 4], in_=t[:])
 
         plan = {}
 
@@ -347,25 +309,21 @@ def tile_fish_zone_bycatch_t2_kernel(
                     at(s + 1 + q // 2, "group", group_h1, c, h, q, "s")
                 at(s + 2, "quant", quant_h1, c, h, 0, 2)
                 at(s + 3, "quant", quant_h1, c, h, 2, 4)
-        TURN = (11, 15, 19, 24, 28, 32)
-        FIRST = 20
-        for u in range(6):
+        FIRST = 16
+        for u in range(4):
             c, half = divmod(u, 2)
+            for q in range(4):
+                s = FIRST + 4 * u + q
+                at(s, "prey", prey, c, half, q)
+                at(s, "eaten", scale_eaten, c, half, q)
             for t in range(4):
-                at(TURN[u], "turn", transpose_h1, c, 4 * half + t)
-                at(TURN[u], "copy", copy_h1, c, 4 * half + t, "v" if t % 2 and u > 2 else "s")
-            if u < 4:
-                for q in range(4):
-                    s = FIRST + 4 * u + q
-                    at(s, "prey", prey, c, half, q)
-                    at(s, "eaten", scale_eaten, c, half, q)
-                at(s + 1, "h2", h2, c, half, 0, 256)
-                at(s + 2, "h2", h2, c, half, 256, 256)
-                at(s + 2, "h2", quant_h2, c, half, 0, 256)
-                at(s + 3, "h2", quant_h2, c, half, 256, 256)
+                i = 4 * half + t
+                at(s + 1, "turn", transpose_h1, c, i)
+                at(s + 1 + t // 2, "h2", h2, c, i)
+                at(s + 2 + t // 2, "quant", quant_h2, c, i)
 
         def emit(step):
-            for stage in ("turn", "move", "prey", "copy", "group", "eaten", "h2", "h1", "quant"):
+            for stage in ("turn", "move", "prey", "group", "eaten", "h2", "h1", "quant"):
                 for fn, args in plan.get((step, stage), []):
                     fn(*args)
 
@@ -398,27 +356,27 @@ def tile_fish_zone_bycatch_t2_kernel(
             quant_x(n + 1)
         for s in range(5, FIRST + 16):
             emit(s)
-        PRE = 2
-        for j in range(PRE):
-            prey_narrow(2, j)
-            scale_narrow(2, j)
-        for j in range(8):
-            if j < 3:
-                emit(FIRST + 16 + j)
-            if j + PRE < 8:
-                prey_narrow(2, j + PRE)
-                scale_narrow(2, j + PRE)
-            expose(j, 0)
-            expose(j, 1)
-            if j >= 2:
-                expose(j - 2, 2)
-            h2(2, j // 4, 128 * (j % 4), 128)
-            if j > 0:
-                quant_h2(2, (j - 1) // 4, 128 * ((j - 1) % 4), 128)
-            if j >= 3:
-                finish(j - 3)
-        quant_h2(2, 1, 384, 128)
-        for j in (6, 7):
-            expose(j, 2)
-        for j in (5, 6, 7):
-            finish(j)
+        for q in range(4):
+            prey(2, 0, q)
+            scale_eaten(2, 0, q)
+            emit(FIRST + 16 + q)
+        for t in range(4):
+            transpose_h1(2, t)
+        for q in range(4):
+            prey(2, 1, q)
+            scale_eaten(2, 1, q)
+            h2(2, q)
+            if q > 0:
+                quant_h2(2, q - 1)
+        for t in range(4):
+            transpose_h1(2, 4 + t)
+        h2(2, 4)
+        quant_h2(2, 3)
+        for t in range(4):
+            if t < 3:
+                h2(2, 5 + t)
+            quant_h2(2, 4 + t)
+        for i in range(8):
+            for c in range(3):
+                expose(i, c)
+            finish(i)

@@ -40,8 +40,8 @@ def tile_fish_zone_bycatch_t2_kernel(
 
         ident = keep.tile([P, P], F32, name="ident", align_bytes=64)
         x_sb = [keep.tile([P, 1536], BF16, name="x%d" % i, align_bytes=64) for i in range(NI)]
-        x_codes = [keep.tile([P, 384], U32, name="xc%d" % i, align_bytes=64) for i in range(NI)]
-        x_sc = [keep.tile([P, 384], U8, name="xs%d" % i, align_bytes=64) for i in range(NI)]
+        x_codes = [keep.tile([P, 768], U32, name="xc%d" % i, align_bytes=64) for i in range(4)]
+        x_sc = [keep.tile([P, 768], U8, name="xs%d" % i, align_bytes=64) for i in range(4)]
         a_w = [keep.tile([P, 3072], U8, name="aw%d" % c, align_bytes=64) for c in range(NC)]
         a_s = keep.tile([P, 4608], U8, name="a_s", align_bytes=64)
         b_w = keep.tile([P, 4096], U8, name="b_w", align_bytes=64)
@@ -80,38 +80,40 @@ def tile_fish_zone_bycatch_t2_kernel(
                 in_=aw_view[:, :, 256 * c : 256 * (c + 1)],
             )
 
-        def load_scales(queue, plane, scales, groups):
+        def load_scales(queue, plane, scales, groups, lo, hi):
             src = scales.bitcast(I32).rearrange("g r w -> r g w")
+            dst = plane[:].bitcast(I32).rearrange("r (g w) -> r g w", g=groups)
             for q in range(4):
-                queue.dma_start(
-                    out=plane[32 * q : 32 * q + 4, :].bitcast(I32).rearrange("r (g w) -> r g w", g=groups),
-                    in_=src[4 * q : 4 * q + 4],
-                )
+                queue.dma_start(out=dst[32 * q : 32 * q + 4, :, lo:hi], in_=src[4 * q : 4 * q + 4, :, lo:hi])
 
-        nc.vector.memset(a_s[:].bitcast(U32), 0)
-        nc.gpsimd.memset(b_s[:].bitcast(U32), 0)
-        nc.gpsimd.memset(e_s[:].bitcast(U32), 0)
         make_identity(nc, ident[:])
+        warm = keep.tile([P, 1], F32, name="warm")
+        nc.vector.memset(warm[:], 0.0)
+        nc.vector.memset(a_s[:].bitcast(U32), 0)
+        nc.vector.memset(b_s[:].bitcast(U32), 0)
+        nc.vector.memset(e_s[:].bitcast(U32), 0)
+        nc.scalar.activation(out=warm[:], in_=warm[:], func=COPY, scale=1.0)
         for g in range(3):
             nc.sync.dma_start(out=x_sb[0][:, 512 * g : 512 * (g + 1)], in_=x_view[0, 0][:, 512 * g : 512 * (g + 1)])
         load_x(1)
-        load_scales(nc.scalar, a_s, move_scales, 3)
+        load_scales(nc.scalar, a_s, move_scales, 3, 0, 128)
         nc.scalar.dma_start(
             out=mob_b[:].rearrange("p (h t) -> p h t", h=2),
             in_=mobility.rearrange("(h p t) -> p h t", p=P, t=4),
         )
         load_a(0)
+        load_a(1)
+        load_scales(nc.scalar, a_s, move_scales, 3, 128, 384)
         for i in range(2, NI):
             load_x(i)
         nc.sync.dma_start(
             out=ov_b[:].rearrange("p (c t) -> p c t", c=3),
             in_=overlap.rearrange("(c p t) -> p c t", p=P, t=4),
         )
-        load_a(1)
-        nc.sync.dma_start(out=b_w[:].bitcast(I32).rearrange("p (g w) -> p g w", g=2), in_=bw_view)
-        load_scales(nc.sync, b_s, prey_scales, 2)
         load_a(2)
-        load_scales(nc.sync, e_s, effort_scales, 3)
+        nc.sync.dma_start(out=b_w[:].bitcast(I32).rearrange("p (g w) -> p g w", g=2), in_=bw_view)
+        load_scales(nc.sync, b_s, prey_scales, 2, 0, 256)
+        load_scales(nc.sync, e_s, effort_scales, 3, 0, 128)
         nc.sync.dma_start(out=e_w[:].bitcast(I32).rearrange("p (g w) -> p g w", g=3), in_=ew_view)
         nc.sync.dma_start(
             out=catch[:].rearrange("p (h w) -> p h w", h=2),
@@ -125,14 +127,16 @@ def tile_fish_zone_bycatch_t2_kernel(
         xbank = {}
         xg = {}
 
-        def permute_x(i, lo, hi):
+        def permute_x(i, lo, hi, engine):
             if lo == 0:
                 t = work.tile([P, 2, 384], F32, name="xw", align_bytes=64, bufs=4)
                 xw[i] = t
-            nc.vector.tensor_copy(
-                out=xw[i][:, :, 128 * lo : 128 * hi],
-                in_=x_sb[i][:, 512 * lo : 512 * hi].bitcast(F32).rearrange("s (w u) -> s u w", u=2),
-            )
+            dst = xw[i][:, :, 128 * lo : 128 * hi]
+            src = x_sb[i][:, 512 * lo : 512 * hi].bitcast(F32).rearrange("s (w u) -> s u w", u=2)
+            if engine == "v":
+                nc.vector.tensor_copy(out=dst, in_=src)
+            else:
+                nc.scalar.copy(out=dst, in_=src)
 
         def transpose_x(i):
             j = i % 2
@@ -148,14 +152,17 @@ def tile_fish_zone_bycatch_t2_kernel(
                     nc.tensor.transpose(dst, xw[i][:, u, 128 * g : 128 * (g + 1)], ident[:])
 
         def copy_x(i, part, engine):
+            pair, j = divmod(i, 2)
+            if j == 0 and part == 0:
+                t = work.tile([P, 3072], BF16, name="xg", align_bytes=64, bufs=2)
+                xg[pair] = t
+            base = 1536 * j
             if part == 0:
-                t = work.tile([P, 1536], BF16, name="xg", align_bytes=64, bufs=4)
-                xg[i] = t
-                dst = t[:, :1024].bitcast(F32).rearrange("z (g s u) -> z g s u", g=2, u=2)
+                dst = xg[pair][:, base : base + 1024].bitcast(F32).rearrange("z (g s u) -> z g s u", g=2, u=2)
                 src = xbank[i][0][:].rearrange("z (g u s) -> z g s u", g=2, u=2)
             else:
-                dst = xg[i][:, 1024:].bitcast(F32).rearrange("z (s u) -> z s u", u=2)
-                src = xbank[i][1][:, 256 * (i % 2) : 256 * (i % 2) + 256].rearrange("z (u s) -> z s u", u=2)
+                dst = xg[pair][:, base + 1024 : base + 1536].bitcast(F32).rearrange("z (s u) -> z s u", u=2)
+                src = xbank[i][1][:, 256 * j : 256 * (j + 1)].rearrange("z (u s) -> z s u", u=2)
             if engine == "v":
                 nc.vector.tensor_copy(out=dst, in_=src)
             else:
@@ -164,9 +171,8 @@ def tile_fish_zone_bycatch_t2_kernel(
         def quant(codes, scales, src):
             nc.vector.quantize_mx(out=codes.bitcast(FP8X4), scales=scales, in_=src)
 
-        def quant_x(i):
-            for lo, hi in ((0, 256), (256, 384)):
-                quant(x_codes[i][:, lo:hi], x_sc[i][:, lo:hi], xg[i][:, 4 * lo : 4 * hi])
+        def quant_x(pair, lo, hi):
+            quant(x_codes[pair][:, lo:hi], x_sc[pair][:, lo:hi], xg[pair][:, 4 * lo : 4 * hi])
 
         s1 = {}
         hf = {}
@@ -175,11 +181,11 @@ def tile_fish_zone_bycatch_t2_kernel(
         def move(c, i):
             ps = bank()
             for g in range(3):
-                cols = slice(128 * g, 128 * (g + 1))
+                cols = slice(384 * (i % 2) + 128 * g, 384 * (i % 2) + 128 * (g + 1))
                 nc.tensor.matmul_mx(
                     out=ps[:],
-                    lhsT=x_codes[i][:, cols].bitcast(FP8X4),
-                    lhsT_scale=x_sc[i][:, cols],
+                    lhsT=x_codes[i // 2][:, cols].bitcast(FP8X4),
+                    lhsT_scale=x_sc[i // 2][:, cols],
                     rhs=a_w[c][:, 1024 * g : 1024 * (g + 1)].bitcast(FP4X4),
                     rhs_scale=a_s[:, 1536 * g + 512 * c : 1536 * g + 512 * (c + 1)],
                     start=(g == 0),
@@ -193,10 +199,10 @@ def tile_fish_zone_bycatch_t2_kernel(
                 full = work.tile([P, 2048], F32, name="hf", align_bytes=64, bufs=6)
                 hf[c, h] = full
             nc.vector.scalar_tensor_tensor(
-                out=hf[c, h][:, 512 * t : 512 * (t + 1)].rearrange("s (t p) -> s t p", t=4),
-                in0=s1[c, i][:].rearrange("s (p t) -> s t p", t=4),
+                out=hf[c, h][:, 512 * t : 512 * (t + 1)].rearrange("s (q p) -> s p q", q=4),
+                in0=s1[c, i][:].rearrange("s (p q) -> s p q", q=4),
                 scalar=mob[:, i : i + 1],
-                in1=x_sb[i][:, 512 * c : 512 * (c + 1)].rearrange("s (p t) -> s t p", t=4),
+                in1=x_sb[i][:, 512 * c : 512 * (c + 1)].rearrange("s (p q) -> s p q", q=4),
                 op0=MULT,
                 op1=ADD,
             )
@@ -205,8 +211,8 @@ def tile_fish_zone_bycatch_t2_kernel(
             if q == 0:
                 t = work.tile([P, 2048], BF16, name="hg", align_bytes=64, bufs=2)
                 hg[c, h] = t
-            dst = hg[c, h][:, 512 * q : 512 * (q + 1)].rearrange("s (z t) -> s z t", t=4)
-            src = hf[c, h][:].rearrange("s (t z) -> s z t", t=4)[:, 128 * q : 128 * (q + 1), :]
+            dst = hg[c, h][:, 512 * q : 512 * (q + 1)].rearrange("s (n i t) -> s n t i", i=4, t=4)
+            src = hf[c, h][:].rearrange("s (t n i) -> s n t i", t=4, i=4)[:, 32 * q : 32 * (q + 1)]
             if engine == "v":
                 nc.vector.tensor_copy(out=dst, in_=src)
             else:
@@ -252,26 +258,31 @@ def tile_fish_zone_bycatch_t2_kernel(
                 t = work.tile([P, 2048], F32, name="eaten", align_bytes=64, bufs=3)
                 eaten[c, half] = t
             nc.scalar.activation(
-                out=eaten[c, half][:, 512 * q : 512 * (q + 1)].rearrange("z (t p) -> z t p", t=4),
-                in_=s2[c, half, q][:].rearrange("z (p t) -> z t p", t=4),
+                out=eaten[c, half][:, 512 * q : 512 * (q + 1)].rearrange("z (t p) -> z p t", t=4),
+                in_=s2[c, half, q][:].rearrange("z (p t) -> z p t", t=4),
                 func=COPY,
                 scale=ov[:, 4 * c + q : 4 * c + q + 1],
             )
 
         def h2(c, i):
             half, t = divmod(i, 4)
-            tile = work.tile([P, 512], BF16, name="h2b", align_bytes=64, bufs=4)
+            if i % 2 == 0:
+                tile = work.tile([P, 1024], BF16, name="h2b", align_bytes=64, bufs=3)
+                h2b[c, i // 2] = tile
             nc.vector.tensor_tensor(
-                out=tile[:].rearrange("z (p q) -> z p q", q=4),
-                in0=tb[c, i][:].rearrange("z (q p) -> z p q", q=4),
-                in1=eaten[c, half][:].rearrange("z (q t p) -> z t p q", q=4, t=4)[:, t],
+                out=h2b[c, i // 2][:, 512 * (i % 2) : 512 * (i % 2 + 1)].rearrange("z (n i q) -> z n q i", i=4, q=4),
+                in0=tb[c, i][:].rearrange("z (q n i) -> z n q i", q=4, i=4),
+                in1=eaten[c, half][:].rearrange("z (q t n i) -> z t n q i", q=4, t=4, i=4)[:, t],
                 op=ADD,
             )
-            h2b[c, i] = tile
 
-        def quant_h2(c, i):
-            cols = slice(128 * i, 128 * (i + 1))
-            quant(h2_codes[c][:, cols], h2_sc[c][:, cols], h2b[c, i][:])
+        def quant_h2(c, lo, hi):
+            base = 512 * (lo % 2)
+            quant(
+                h2_codes[c][:, 128 * lo : 128 * hi],
+                h2_sc[c][:, 128 * lo : 128 * hi],
+                h2b[c, lo // 2][:, base : base + 512 * (hi - lo)],
+            )
 
         s3 = {}
 
@@ -288,10 +299,16 @@ def tile_fish_zone_bycatch_t2_kernel(
                 stop=(c == 2),
             )
 
-        def finish(j):
+        def finish(j, pieces=1):
             t = work.tile([P, NF], F32, name="res", align_bytes=64, bufs=8)
-            nc.vector.tensor_tensor(out=t[:], in0=s3[j][:], in1=catch[:, NF * j : NF * (j + 1)], op=MULT)
-            nc.sync.dma_start(out=out_view[j // 4, j % 4], in_=t[:])
+            w = NF // pieces
+            for n in range(pieces):
+                cols = slice(n * w, (n + 1) * w)
+                nc.vector.tensor_tensor(
+                    out=t[:, cols], in0=s3[j][:, cols], in1=catch[:, NF * j + n * w : NF * j + (n + 1) * w], op=MULT
+                )
+                queue = nc.sync if n % 2 == 0 else nc.scalar
+                queue.dma_start(out=out_view[j // 4, j % 4][:, cols], in_=t[:, cols])
 
         plan = {}
 
@@ -300,16 +317,19 @@ def tile_fish_zone_bycatch_t2_kernel(
 
         for c in range(NC):
             for k in range(NI):
-                s = NI * c + k
+                s = 2 * k + c if c < 2 else 16 + k
                 at(s, "move", move, c, k)
                 at(s, "h1", h1, c, k)
-            for h in range(2):
-                s = NI * c + 4 * h + 3
-                for q in range(4):
-                    at(s + 1 + q // 2, "group", group_h1, c, h, q, "s")
-                at(s + 2, "quant", quant_h1, c, h, 0, 2)
-                at(s + 3, "quant", quant_h1, c, h, 2, 4)
-        FIRST = 16
+                if k % 4 == 3:
+                    h = k // 4
+                    for q in range(4):
+                        at(s + 1 + q // 2, "group", group_h1, c, h, q, "s")
+                    if (c, h) == (2, 1):
+                        at(s + 1, "quant", quant_h1, c, h, 0, 2)
+                        at(s + 2, "quant", quant_h1, c, h, 2, 4)
+                    else:
+                        at(s + 3, "quant", quant_h1, c, h, 0, 4)
+        FIRST = 20
         for u in range(4):
             c, half = divmod(u, 2)
             for q in range(4):
@@ -320,7 +340,8 @@ def tile_fish_zone_bycatch_t2_kernel(
                 i = 4 * half + t
                 at(s + 1, "turn", transpose_h1, c, i)
                 at(s + 1 + t // 2, "h2", h2, c, i)
-                at(s + 2 + t // 2, "quant", quant_h2, c, i)
+                if t % 2 == 1:
+                    at(s + 2 + t // 2, "quant", quant_h2, c, i - 1, i + 1)
 
         def emit(step):
             for stage in ("turn", "move", "prey", "group", "eaten", "h2", "h1", "quant"):
@@ -328,33 +349,37 @@ def tile_fish_zone_bycatch_t2_kernel(
                     fn(*args)
 
         for g in range(3):
-            permute_x(0, g, g + 1)
-        permute_x(1, 0, 3)
+            permute_x(0, g, g + 1, "v")
+        permute_x(1, 0, 3, "v")
         transpose_x(0)
         transpose_x(1)
         copy_x(0, 0, "s")
         copy_x(0, 1, "v")
         copy_x(1, 0, "s")
-        quant_x(0)
+        quant_x(0, 0, 256)
+        quant_x(0, 256, 384)
         copy_x(1, 1, "s")
-        permute_x(2, 0, 3)
-        permute_x(3, 0, 3)
-        quant_x(1)
+        permute_x(2, 0, 3, "v")
+        permute_x(3, 0, 3, "v")
+        quant_x(0, 384, 640)
+        quant_x(0, 640, 768)
         emit(0)
-        for n, runs in ((2, (1,)), (4, (2,)), (6, (3, 4))):
-            for i in (n, n + 1):
+        emit(1)
+        for pair in (1, 2, 3):
+            for i in (2 * pair, 2 * pair + 1):
                 transpose_x(i)
-            for i in (n, n + 1):
+            for i in (2 * pair, 2 * pair + 1):
                 copy_x(i, 0, "s")
                 copy_x(i, 1, "s")
-            if n < 6:
-                permute_x(n + 2, 0, 3)
-                permute_x(n + 3, 0, 3)
-            for s in runs:
+            if pair < 3:
+                permute_x(2 * pair + 2, 0, 3, "v")
+                permute_x(2 * pair + 3, 0, 3, "s")
+            for s in ((2, 3), (4, 5), (6, 7, 8, 9))[pair - 1]:
                 emit(s)
-            quant_x(n)
-            quant_x(n + 1)
-        for s in range(5, FIRST + 16):
+                if s == 2 * pair:
+                    quant_x(pair, 0, 512)
+                    quant_x(pair, 512, 768)
+        for s in range(10, FIRST + 16):
             emit(s)
         for q in range(4):
             prey(2, 0, q)
@@ -366,17 +391,16 @@ def tile_fish_zone_bycatch_t2_kernel(
             prey(2, 1, q)
             scale_eaten(2, 1, q)
             h2(2, q)
-            if q > 0:
-                quant_h2(2, q - 1)
+            if q % 2 == 1:
+                quant_h2(2, q - 1, q + 1)
         for t in range(4):
             transpose_h1(2, 4 + t)
         h2(2, 4)
-        quant_h2(2, 3)
         for t in range(4):
             if t < 3:
                 h2(2, 5 + t)
-            quant_h2(2, 4 + t)
+            quant_h2(2, 4 + t, 5 + t)
         for i in range(8):
             for c in range(3):
                 expose(i, c)
-            finish(i)
+            finish(i, 2 if i == 7 else 1)

@@ -97,31 +97,30 @@ def tile_fish_zone_bycatch_t2_kernel(
             nc.sync.dma_start(out=x_sb[0][:, 512 * g : 512 * (g + 1)], in_=x_view[0, 0][:, 512 * g : 512 * (g + 1)])
         load_x(1)
         load_scales(nc.scalar, a_s, move_scales, 3, 0, 128)
-        nc.scalar.dma_start(
+        load_a(0)
+        load_a(1)
+        load_scales(nc.sync, a_s, move_scales, 3, 128, 384)
+        nc.sync.dma_start(
             out=mob_b[:].rearrange("p (h t) -> p h t", h=2),
             in_=mobility.rearrange("(h p t) -> p h t", p=P, t=4),
         )
-        load_a(0)
-        load_a(1)
-        load_scales(nc.scalar, a_s, move_scales, 3, 128, 384)
         for i in range(2, NI):
             load_x(i)
         nc.sync.dma_start(
             out=ov_b[:].rearrange("p (c t) -> p c t", c=3),
             in_=overlap.rearrange("(c p t) -> p c t", p=P, t=4),
         )
+        nc.gpsimd.tensor_copy(out=mob[:], in_=mob_b[:])
+        nc.gpsimd.tensor_copy(out=ov[:], in_=ov_b[:])
         load_a(2)
-        nc.sync.dma_start(out=b_w[:].bitcast(I32).rearrange("p (g w) -> p g w", g=2), in_=bw_view)
         load_scales(nc.sync, b_s, prey_scales, 2, 0, 256)
+        nc.sync.dma_start(out=b_w[:].bitcast(I32).rearrange("p (g w) -> p g w", g=2), in_=bw_view)
         load_scales(nc.sync, e_s, effort_scales, 3, 0, 128)
         nc.sync.dma_start(out=e_w[:].bitcast(I32).rearrange("p (g w) -> p g w", g=3), in_=ew_view)
         nc.sync.dma_start(
             out=catch[:].rearrange("p (h w) -> p h w", h=2),
             in_=catchability.rearrange("(h p t) f -> p h (t f)", p=P, t=4),
         )
-
-        nc.gpsimd.tensor_copy(out=mob[:], in_=mob_b[:])
-        nc.gpsimd.tensor_copy(out=ov[:], in_=ov_b[:])
 
         xw = {}
         xbank = {}
@@ -131,8 +130,8 @@ def tile_fish_zone_bycatch_t2_kernel(
             if lo == 0:
                 t = work.tile([P, 2, 384], F32, name="xw", align_bytes=64, bufs=4)
                 xw[i] = t
-            dst = xw[i][:, :, 128 * lo : 128 * hi]
-            src = x_sb[i][:, 512 * lo : 512 * hi].bitcast(F32).rearrange("s (w u) -> s u w", u=2)
+            dst = xw[i][:].rearrange("s u w -> s w u")[:, 128 * lo : 128 * hi]
+            src = x_sb[i][:, 512 * lo : 512 * hi].bitcast(F32).rearrange("s (w u) -> s w u", u=2)
             if engine == "v":
                 nc.vector.tensor_copy(out=dst, in_=src)
             else:
@@ -140,7 +139,7 @@ def tile_fish_zone_bycatch_t2_kernel(
 
         def transpose_x(i):
             j = i % 2
-            if j == 0:
+            if j == 0 or i == 1:
                 xbank["shared"] = bank()
             xbank[i] = (bank(), xbank["shared"])
             for g in range(3):
@@ -320,15 +319,12 @@ def tile_fish_zone_bycatch_t2_kernel(
                 s = 2 * k + c if c < 2 else 16 + k
                 at(s, "move", move, c, k)
                 at(s, "h1", h1, c, k)
-                if k % 4 == 3:
-                    h = k // 4
-                    for q in range(4):
-                        at(s + 1 + q // 2, "group", group_h1, c, h, q, "s")
-                    if (c, h) == (2, 1):
-                        at(s + 1, "quant", quant_h1, c, h, 0, 2)
-                        at(s + 2, "quant", quant_h1, c, h, 2, 4)
-                    else:
-                        at(s + 3, "quant", quant_h1, c, h, 0, 4)
+        GROUP = (8, 12, 15, 18, 23, 27)
+        for n in range(6):
+            c, h = ((0, 0), (1, 0), (0, 1), (1, 1), (2, 0), (2, 1))[n]
+            for q in range(4):
+                at(GROUP[n] + q // 2, "group", group_h1, c, h, q, "s")
+            at(GROUP[n] + 3, "quant", quant_h1, c, h, 0, 4)
         FIRST = 20
         for u in range(4):
             c, half = divmod(u, 2)
@@ -339,9 +335,9 @@ def tile_fish_zone_bycatch_t2_kernel(
             for t in range(4):
                 i = 4 * half + t
                 at(s + 1, "turn", transpose_h1, c, i)
-                at(s + 1 + t // 2, "h2", h2, c, i)
+                at(s + 2 + t // 2, "h2", h2, c, i)
                 if t % 2 == 1:
-                    at(s + 2 + t // 2, "quant", quant_h2, c, i - 1, i + 1)
+                    at(s + 3 + t // 2, "quant", quant_h2, c, i - 1, i + 1)
 
         def emit(step):
             for stage in ("turn", "move", "prey", "group", "eaten", "h2", "h1", "quant"):

@@ -298,16 +298,49 @@ def tile_fish_zone_bycatch_t2_kernel(
                 stop=(c == 2),
             )
 
-        def finish(j, pieces=1):
+        late = {}
+
+        def finish_late(j):
+            raw = work.tile([P, NF], F32, name="raw", align_bytes=64, bufs=2)
             t = work.tile([P, NF], F32, name="res", align_bytes=64, bufs=8)
-            w = NF // pieces
-            for n in range(pieces):
-                cols = slice(n * w, (n + 1) * w)
+            nc.scalar.copy(out=raw[:], in_=s3[j][:])
+            nc.gpsimd.tensor_tensor(out=t[:], in0=raw[:], in1=catch[:, NF * j : NF * (j + 1)], op=MULT)
+            late[j] = t
+
+        def store_late(j):
+            nc.scalar.dma_start(out=out_view[j // 4, j % 4], in_=late[j][:])
+
+        def expose_split(j):
+            for half in range(2):
+                ps = bank()
+                for n in range(2):
+                    col = 256 * half + 128 * n
+                    for c in range(3):
+                        nc.tensor.matmul_mx(
+                            out=ps[:, 128 * n : 128 * (n + 1)],
+                            lhsT=h2_codes[c][:, 128 * j : 128 * (j + 1)].bitcast(FP8X4),
+                            lhsT_scale=h2_sc[c][:, 128 * j : 128 * (j + 1)],
+                            rhs=e_w[:, 1024 * c + 2 * col : 1024 * c + 2 * col + 256].bitcast(FP4X4),
+                            rhs_scale=e_s[:, 512 * c + col : 512 * c + col + 128],
+                            start=(c == 0),
+                            stop=(c == 2),
+                        )
+                s3[j, half] = ps
+
+        def finish_split(j):
+            for half in range(2):
+                t = work.tile([P, 256], F32, name="res2", align_bytes=64, bufs=2)
+                cols = slice(256 * half, 256 * (half + 1))
                 nc.vector.tensor_tensor(
-                    out=t[:, cols], in0=s3[j][:, cols], in1=catch[:, NF * j + n * w : NF * j + (n + 1) * w], op=MULT
+                    out=t[:], in0=s3[j, half][:, :256], in1=catch[:, NF * j + 256 * half : NF * j + 256 * (half + 1)], op=MULT
                 )
-                queue = nc.sync if n % 2 == 0 else nc.scalar
-                queue.dma_start(out=out_view[j // 4, j % 4][:, cols], in_=t[:, cols])
+                queue = nc.sync if half == 0 else nc.scalar
+                queue.dma_start(out=out_view[j // 4, j % 4][:, cols], in_=t[:])
+
+        def finish(j):
+            t = work.tile([P, NF], F32, name="res", align_bytes=64, bufs=8)
+            nc.vector.tensor_tensor(out=t[:], in0=s3[j][:], in1=catch[:, NF * j : NF * (j + 1)], op=MULT)
+            nc.sync.dma_start(out=out_view[j // 4, j % 4], in_=t[:])
 
         plan = {}
 
@@ -316,16 +349,16 @@ def tile_fish_zone_bycatch_t2_kernel(
 
         for c in range(NC):
             for k in range(NI):
-                s = 2 * k + c if c < 2 else 16 + k
+                s = (2 * k + c if k < 4 else 4 + 4 * c + k) if c < 2 else 16 + k
                 at(s, "move", move, c, k)
                 at(s, "h1", h1, c, k)
-        GROUP = (8, 12, 15, 18, 23, 27)
+        GROUP = (8, 10, 12, 17, 21, 25)
         for n in range(6):
             c, h = ((0, 0), (1, 0), (0, 1), (1, 1), (2, 0), (2, 1))[n]
             for q in range(4):
                 at(GROUP[n] + q // 2, "group", group_h1, c, h, q, "s")
             at(GROUP[n] + 3, "quant", quant_h1, c, h, 0, 4)
-        FIRST = 20
+        FIRST = 18
         for u in range(4):
             c, half = divmod(u, 2)
             for q in range(4):
@@ -370,9 +403,9 @@ def tile_fish_zone_bycatch_t2_kernel(
             if pair < 3:
                 permute_x(2 * pair + 2, 0, 3, "v")
                 permute_x(2 * pair + 3, 0, 3, "s")
-            for s in ((2, 3), (4, 5), (6, 7, 8, 9))[pair - 1]:
+            for s in ((2, 3), (4, 5, 6), (7, 8, 9))[pair - 1]:
                 emit(s)
-                if s == 2 * pair:
+                if s == (2, 4, 7)[pair - 1]:
                     quant_x(pair, 0, 512)
                     quant_x(pair, 512, 768)
         for s in range(10, FIRST + 16):
@@ -396,7 +429,14 @@ def tile_fish_zone_bycatch_t2_kernel(
             if t < 3:
                 h2(2, 5 + t)
             quant_h2(2, 4 + t, 5 + t)
-        for i in range(8):
+        for i in range(7):
             for c in range(3):
                 expose(i, c)
-            finish(i, 2 if i == 7 else 1)
+            if i in (0, 2, 4):
+                finish_late(i)
+            else:
+                finish(i)
+            if i - 2 in (0, 2, 4):
+                store_late(i - 2)
+        expose_split(7)
+        finish_split(7)

from contextlib import ExitStack

import concourse.mybir as mybir
from concourse.masks import make_identity

FLOPS = 2 * 1024 * 1536 * 1536 + 2 * 1024 * 1024 * 1536 + 2 * 1024 * 1536 * 512

F32 = mybir.dt.float32
BF16 = mybir.dt.bfloat16
I32 = mybir.dt.int32
U32 = mybir.dt.uint32
U8 = mybir.dt.uint8
FP8X4 = mybir.dt.float8_e4m3fn_x4
FP4X4 = mybir.dt.float4_e2m1fn_x4
MULT = mybir.AluOpType.mult
ADD = mybir.AluOpType.add
COPY = mybir.ActivationFunctionType.Copy

P = 128
NC = 3
NI = 8
NF = 512


def tile_fish_zone_bycatch_t2_kernel(
    tc, stocks, move_words, move_scales, mobility, prey_words, prey_scales, overlap,
    effort_words, effort_scales, catchability, out,
):
    nc = tc.nc
    with ExitStack() as ctx:
        keep = ctx.enter_context(tc.tile_pool(name="keep", bufs=1))
        work = ctx.enter_context(tc.tile_pool(name="work", bufs=2))
        psum = ctx.enter_context(tc.psum_pool(name="psum", bufs=8))

        def bank():
            t = psum.tile([P, 512], F32, name="bank")
            return t

        ctx.enter_context(tc.manual_schedule())

        ident = keep.tile([P, P], F32, name="ident", align_bytes=64)
        x_sb = [keep.tile([P, 1536], BF16, name="x%d" % i, align_bytes=64) for i in range(NI)]
        x_codes = [keep.tile([P, 768], U32, name="xc%d" % i, align_bytes=64) for i in range(4)]
        x_sc = [keep.tile([P, 768], U8, name="xs%d" % i, align_bytes=64) for i in range(4)]
        a_w = [keep.tile([P, 3072], U8, name="aw%d" % c, align_bytes=64) for c in range(NC)]
        a_s = keep.tile([P, 4608], U8, name="a_s", align_bytes=64)
        b_w = keep.tile([P, 4096], U8, name="b_w", align_bytes=64)
        b_s = keep.tile([P, 2048], U8, name="b_s", align_bytes=64)
        e_w = keep.tile([P, 3072], U8, name="e_w", align_bytes=64)
        e_s = keep.tile([P, 1536], U8, name="e_s", align_bytes=64)
        mob_b = keep.tile([P, NI], BF16, name="mob_b")
        ov_b = keep.tile([P, 12], BF16, name="ov_b")
        mob = keep.tile([P, NI], F32, name="mob")
        ov = keep.tile([P, 12], F32, name="ov")
        catch = keep.tile([P, NI * NF], BF16, name="catch", align_bytes=64)
        h1_codes = {}
        h1_sc = {}
        h2_codes = {}
        h2_sc = {}
        for c in range(NC):
            for h in range(2):
                h1_codes[c, h] = keep.tile([P, 512], U32, name="h1c%d%d" % (c, h), align_bytes=64)
                h1_sc[c, h] = keep.tile([P, 512], U8, name="h1s%d%d" % (c, h), align_bytes=64)
            h2_codes[c] = keep.tile([P, 1024], U32, name="h2c%d" % c, align_bytes=64)
            h2_sc[c] = keep.tile([P, 1024], U8, name="h2s%d" % c, align_bytes=64)

        out_view = out.rearrange("(h p t) f -> h t p f", p=P, t=4)

        x_view = stocks.rearrange("(h p t) z -> h t p z", p=P, t=4)
        aw_view = move_words.bitcast(I32).rearrange("g p w -> p g w")
        bw_view = prey_words.bitcast(I32).rearrange("g p w -> p g w")
        ew_view = effort_words.bitcast(I32).rearrange("g p w -> p g w")

        def load_x(i):
            nc.sync.dma_start(out=x_sb[i][:], in_=x_view[i // 4, i % 4])

        def load_a(c):
            nc.sync.dma_start(
                out=a_w[c][:].bitcast(I32).rearrange("p (g w) -> p g w", g=3),
                in_=aw_view[:, :, 256 * c : 256 * (c + 1)],
            )

        def load_scales(queue, plane, scales, groups, lo, hi):
            src = scales.bitcast(I32).rearrange("g r w -> r g w")
            dst = plane[:].bitcast(I32).rearrange("r (g w) -> r g w", g=groups)
            for q in range(4):
                queue.dma_start(out=dst[32 * q : 32 * q + 4, :, lo:hi], in_=src[4 * q : 4 * q + 4, :, lo:hi])

        make_identity(nc, ident[:])
        warm = keep.tile([P, 1], F32, name="warm")
        nc.vector.memset(warm[:], 0.0)
        nc.vector.memset(a_s[:].bitcast(U32), 0)
        nc.vector.memset(b_s[:].bitcast(U32), 0)
        nc.vector.memset(e_s[:].bitcast(U32), 0)
        nc.scalar.activation(out=warm[:], in_=warm[:], func=COPY, scale=1.0)
        for g in range(3):
            nc.sync.dma_start(out=x_sb[0][:, 512 * g : 512 * (g + 1)], in_=x_view[0, 0][:, 512 * g : 512 * (g + 1)])
        load_x(1)
        load_scales(nc.scalar, a_s, move_scales, 3, 0, 128)
        load_a(0)
        load_a(1)
        load_scales(nc.sync, a_s, move_scales, 3, 128, 384)
        nc.sync.dma_start(
            out=mob_b[:].rearrange("p (h t) -> p h t", h=2),
            in_=mobility.rearrange("(h p t) -> p h t", p=P, t=4),
        )
        for i in range(2, NI):
            load_x(i)
        nc.sync.dma_start(
            out=ov_b[:].rearrange("p (c t) -> p c t", c=3),
            in_=overlap.rearrange("(c p t) -> p c t", p=P, t=4),
        )
        nc.gpsimd.tensor_copy(out=mob[:], in_=mob_b[:])
        nc.gpsimd.tensor_copy(out=ov[:], in_=ov_b[:])
        load_a(2)
        load_scales(nc.sync, b_s, prey_scales, 2, 0, 256)
        nc.sync.dma_start(out=b_w[:].bitcast(I32).rearrange("p (g w) -> p g w", g=2), in_=bw_view)
        load_scales(nc.sync, e_s, effort_scales, 3, 0, 128)
        nc.sync.dma_start(out=e_w[:].bitcast(I32).rearrange("p (g w) -> p g w", g=3), in_=ew_view)
        nc.sync.dma_start(
            out=catch[:].rearrange("p (h w) -> p h w", h=2),
            in_=catchability.rearrange("(h p t) f -> p h (t f)", p=P, t=4),
        )

        xw = {}
        xbank = {}
        xg = {}

        def permute_x(i, lo, hi, engine):
            if lo == 0:
                t = work.tile([P, 2, 384], F32, name="xw", align_bytes=64, bufs=4)
                xw[i] = t
            dst = xw[i][:].rearrange("s u w -> s w u")[:, 128 * lo : 128 * hi]
            src = x_sb[i][:, 512 * lo : 512 * hi].bitcast(F32).rearrange("s (w u) -> s w u", u=2)
            if engine == "v":
                nc.vector.tensor_copy(out=dst, in_=src)
            else:
                nc.scalar.copy(out=dst, in_=src)

        def transpose_x(i):
            j = i % 2
            if j == 0 or i == 1:
                xbank["shared"] = bank()
            xbank[i] = (bank(), xbank["shared"])
            for g in range(3):
                for u in range(2):
                    if g < 2:
                        dst = xbank[i][0][:, 256 * g + 128 * u : 256 * g + 128 * (u + 1)]
                    else:
                        dst = xbank[i][1][:, 256 * j + 128 * u : 256 * j + 128 * (u + 1)]
                    nc.tensor.transpose(dst, xw[i][:, u, 128 * g : 128 * (g + 1)], ident[:])

        def copy_x(i, part, engine):
            pair, j = divmod(i, 2)
            if j == 0 and part == 0:
                t = work.tile([P, 3072], BF16, name="xg", align_bytes=64, bufs=2)
                xg[pair] = t
            base = 1536 * j
            if part == 0:
                dst = xg[pair][:, base : base + 1024].bitcast(F32).rearrange("z (g s u) -> z g s u", g=2, u=2)
                src = xbank[i][0][:].rearrange("z (g u s) -> z g s u", g=2, u=2)
            else:
                dst = xg[pair][:, base + 1024 : base + 1536].bitcast(F32).rearrange("z (s u) -> z s u", u=2)
                src = xbank[i][1][:, 256 * j : 256 * (j + 1)].rearrange("z (u s) -> z s u", u=2)
            if engine == "v":
                nc.vector.tensor_copy(out=dst, in_=src)
            else:
                nc.scalar.copy(out=dst, in_=src)

        def quant(codes, scales, src):
            nc.vector.quantize_mx(out=codes.bitcast(FP8X4), scales=scales, in_=src)

        def quant_x(pair, lo, hi):
            quant(x_codes[pair][:, lo:hi], x_sc[pair][:, lo:hi], xg[pair][:, 4 * lo : 4 * hi])

        s1 = {}
        hf = {}
        hg = {}

        def move(c, i):
            ps = bank()
            for g in range(3):
                cols = slice(384 * (i % 2) + 128 * g, 384 * (i % 2) + 128 * (g + 1))
                nc.tensor.matmul_mx(
                    out=ps[:],
                    lhsT=x_codes[i // 2][:, cols].bitcast(FP8X4),
                    lhsT_scale=x_sc[i // 2][:, cols],
                    rhs=a_w[c][:, 1024 * g : 1024 * (g + 1)].bitcast(FP4X4),
                    rhs_scale=a_s[:, 1536 * g + 512 * c : 1536 * g + 512 * (c + 1)],
                    start=(g == 0),
                    stop=(g == 2),
                )
            s1[c, i] = ps

        def h1(c, i):
            h, t = divmod(i, 4)
            if t == 0:
                full = work.tile([P, 2048], F32, name="hf", align_bytes=64, bufs=6)
                hf[c, h] = full
            nc.vector.scalar_tensor_tensor(
                out=hf[c, h][:, 512 * t : 512 * (t + 1)].rearrange("s (q p) -> s p q", q=4),
                in0=s1[c, i][:].rearrange("s (p q) -> s p q", q=4),
                scalar=mob[:, i : i + 1],
                in1=x_sb[i][:, 512 * c : 512 * (c + 1)].rearrange("s (p q) -> s p q", q=4),
                op0=MULT,
                op1=ADD,
            )

        def group_h1(c, h, q, engine="s"):
            if q == 0:
                t = work.tile([P, 2048], BF16, name="hg", align_bytes=64, bufs=2)
                hg[c, h] = t
            dst = hg[c, h][:, 512 * q : 512 * (q + 1)].rearrange("s (n i t) -> s n t i", i=4, t=4)
            src = hf[c, h][:].rearrange("s (t n i) -> s n t i", t=4, i=4)[:, 32 * q : 32 * (q + 1)]
            if engine == "v":
                nc.vector.tensor_copy(out=dst, in_=src)
            else:
                nc.scalar.copy(out=dst, in_=src)

        def quant_h1(c, h, lo, hi):
            cols = slice(128 * lo, 128 * hi)
            quant(h1_codes[c, h][:, cols], h1_sc[c, h][:, cols], hg[c, h][:, 512 * lo : 512 * hi])

        tb = {}

        def transpose_h1(c, i):
            h, t = divmod(i, 4)
            ps = bank()
            for tz in range(4):
                nc.tensor.transpose(
                    ps[:, 128 * tz : 128 * (tz + 1)],
                    hf[c, h][:, 512 * t + 128 * tz : 512 * t + 128 * (tz + 1)],
                    ident[:],
                )
            tb[c, i] = ps

        s2 = {}
        eaten = {}
        h2b = {}

        def prey(c, half, q):
            ps = bank()
            for g in range(2):
                nc.tensor.matmul_mx(
                    out=ps[:],
                    lhsT=h1_codes[c, g][:, 128 * q : 128 * (q + 1)].bitcast(FP8X4),
                    lhsT_scale=h1_sc[c, g][:, 128 * q : 128 * (q + 1)],
                    rhs=b_w[:, 2048 * g + 1024 * half : 2048 * g + 1024 * (half + 1)].bitcast(FP4X4),
                    rhs_scale=b_s[:, 1024 * g + 512 * half : 1024 * g + 512 * (half + 1)],
                    start=(g == 0),
                    stop=(g == 1),
                )
            s2[c, half, q] = ps

        def scale_eaten(c, half, q):
            if q == 0:
                t = work.tile([P, 2048], F32, name="eaten", align_bytes=64, bufs=3)
                eaten[c, half] = t
            nc.scalar.activation(
                out=eaten[c, half][:, 512 * q : 512 * (q + 1)].rearrange("z (t p) -> z p t", t=4),
                in_=s2[c, half, q][:].rearrange("z (p t) -> z p t", t=4),
                func=COPY,
                scale=ov[:, 4 * c + q : 4 * c + q + 1],
            )

        def h2(c, i):
            half, t = divmod(i, 4)
            if i % 2 == 0:
                tile = work.tile([P, 1024], BF16, name="h2b", align_bytes=64, bufs=3)
                h2b[c, i // 2] = tile
            nc.vector.tensor_tensor(
                out=h2b[c, i // 2][:, 512 * (i % 2) : 512 * (i % 2 + 1)].rearrange("z (n i q) -> z n q i", i=4, q=4),
                in0=tb[c, i][:].rearrange("z (q n i) -> z n q i", q=4, i=4),
                in1=eaten[c, half][:].rearrange("z (q t n i) -> z t n q i", q=4, t=4, i=4)[:, t],
                op=ADD,
            )

        def quant_h2(c, lo, hi):
            base = 512 * (lo % 2)
            quant(
                h2_codes[c][:, 128 * lo : 128 * hi],
                h2_sc[c][:, 128 * lo : 128 * hi],
                h2b[c, lo // 2][:, base : base + 512 * (hi - lo)],
            )

        s3 = {}

        def expose(j, c):
            if c == 0:
                s3[j] = bank()
            nc.tensor.matmul_mx(
                out=s3[j][:],
                lhsT=h2_codes[c][:, 128 * j : 128 * (j + 1)].bitcast(FP8X4),
                lhsT_scale=h2_sc[c][:, 128 * j : 128 * (j + 1)],
                rhs=e_w[:, 1024 * c : 1024 * (c + 1)].bitcast(FP4X4),
                rhs_scale=e_s[:, 512 * c : 512 * (c + 1)],
                start=(c == 0),
                stop=(c == 2),
            )

        late = {}

        def finish_late(j):
            raw = work.tile([P, NF], F32, name="raw", align_bytes=64, bufs=2)
            t = work.tile([P, NF], F32, name="res", align_bytes=64, bufs=8)
            nc.scalar.copy(out=raw[:], in_=s3[j][:])
            nc.gpsimd.tensor_tensor(out=t[:], in0=raw[:], in1=catch[:, NF * j : NF * (j + 1)], op=MULT)
            late[j] = t

        def store_late(j):
            nc.scalar.dma_start(out=out_view[j // 4, j % 4], in_=late[j][:])

        def expose_split(j):
            for half in range(2):
                ps = bank()
                for n in range(2):
                    col = 256 * half + 128 * n
                    for c in range(3):
                        nc.tensor.matmul_mx(
                            out=ps[:, 128 * n : 128 * (n + 1)],
                            lhsT=h2_codes[c][:, 128 * j : 128 * (j + 1)].bitcast(FP8X4),
                            lhsT_scale=h2_sc[c][:, 128 * j : 128 * (j + 1)],
                            rhs=e_w[:, 1024 * c + 2 * col : 1024 * c + 2 * col + 256].bitcast(FP4X4),
                            rhs_scale=e_s[:, 512 * c + col : 512 * c + col + 128],
                            start=(c == 0),
                            stop=(c == 2),
                        )
                s3[j, half] = ps

        def finish_split(j):
            for half in range(2):
                t = work.tile([P, 256], F32, name="res2", align_bytes=64, bufs=2)
                cols = slice(256 * half, 256 * (half + 1))
                nc.vector.tensor_tensor(
                    out=t[:], in0=s3[j, half][:, :256], in1=catch[:, NF * j + 256 * half : NF * j + 256 * (half + 1)], op=MULT
                )
                queue = nc.sync if half == 0 else nc.scalar
                queue.dma_start(out=out_view[j // 4, j % 4][:, cols], in_=t[:])

        def finish(j):
            t = work.tile([P, NF], F32, name="res", align_bytes=64, bufs=8)
            nc.vector.tensor_tensor(out=t[:], in0=s3[j][:], in1=catch[:, NF * j : NF * (j + 1)], op=MULT)
            nc.sync.dma_start(out=out_view[j // 4, j % 4], in_=t[:])

        plan = {}

        def at(step, stage, fn, *args):
            plan.setdefault((step, stage), []).append((fn, args))

        for c in range(NC):
            for k in range(NI):
                s = (2 * k + c if k < 4 else 4 + 4 * c + k) if c < 2 else 16 + k
                at(s, "move", move, c, k)
                at(s, "h1", h1, c, k)
        GROUP = (8, 10, 12, 17, 21, 25)
        for n in range(6):
            c, h = ((0, 0), (1, 0), (0, 1), (1, 1), (2, 0), (2, 1))[n]
            for q in range(4):
                at(GROUP[n] + q // 2, "group", group_h1, c, h, q, "s")
            at(GROUP[n] + 3, "quant", quant_h1, c, h, 0, 4)
        FIRST = 18
        for u in range(4):
            c, half = divmod(u, 2)
            for q in range(4):
                s = FIRST + 4 * u + q
                at(s, "prey", prey, c, half, q)
                at(s, "eaten", scale_eaten, c, half, q)
            for t in range(4):
                i = 4 * half + t
                at(s + 1, "turn", transpose_h1, c, i)
                at(s + 2 + t // 2, "h2", h2, c, i)
                if t % 2 == 1:
                    at(s + 3 + t // 2, "quant", quant_h2, c, i - 1, i + 1)

        def emit(step):
            for stage in ("turn", "move", "prey", "group", "eaten", "h2", "h1", "quant"):
                for fn, args in plan.get((step, stage), []):
                    fn(*args)

        for g in range(3):
            permute_x(0, g, g + 1, "v")
        permute_x(1, 0, 3, "v")
        transpose_x(0)
        transpose_x(1)
        copy_x(0, 0, "s")
        copy_x(0, 1, "v")
        copy_x(1, 0, "s")
        quant_x(0, 0, 256)
        quant_x(0, 256, 384)
        copy_x(1, 1, "s")
        permute_x(2, 0, 3, "v")
        permute_x(3, 0, 3, "v")
        quant_x(0, 384, 640)
        quant_x(0, 640, 768)
        emit(0)
        emit(1)
        for pair in (1, 2, 3):
            for i in (2 * pair, 2 * pair + 1):
                transpose_x(i)
            for i in (2 * pair, 2 * pair + 1):
                copy_x(i, 0, "s")
                copy_x(i, 1, "s")
            if pair < 3:
                permute_x(2 * pair + 2, 0, 3, "v")
                permute_x(2 * pair + 3, 0, 3, "s")
            for s in ((2, 3), (4, 5, 6), (7, 8, 9))[pair - 1]:
                emit(s)
                if s == (2, 4, 7)[pair - 1]:
                    quant_x(pair, 0, 512)
                    quant_x(pair, 512, 768)
        for s in range(10, FIRST + 16):
            emit(s)
        for q in range(4):
            prey(2, 0, q)
            scale_eaten(2, 0, q)
            emit(FIRST + 16 + q)
        for t in range(4):
            transpose_h1(2, t)
        for q in range(4):
            prey(2, 1, q)
            scale_eaten(2, 1, q)
            h2(2, q)
            if q % 2 == 1:
                quant_h2(2, q - 1, q + 1)
        for t in range(4):
            transpose_h1(2, 4 + t)
        h2(2, 4)
        for t in range(4):
            if t < 3:
                h2(2, 5 + t)
            quant_h2(2, 4 + t, 5 + t)
        for i in range(7):
            for c in range(3):
                expose(i, c)
            if i in (0, 2, 4):
                finish_late(i)
            else:
                finish(i)
            if i - 2 in (0, 2, 4):
                store_late(i - 2)
        expose_split(7)
        finish_split(7)
